import numpy as np
import ml_dtypes


def mxq(x, axis, fmt="e4m3"):
    dtype, down = {"e4m3": (ml_dtypes.float8_e4m3fn, 7), "e5m2": (ml_dtypes.float8_e5m2, 14)}[fmt]
    v = np.moveaxis(np.asarray(x, np.float32).astype(ml_dtypes.bfloat16).astype(np.float64), axis, -1)
    blocks = v.reshape(v.shape[:-1] + (-1, 32))
    amax = np.abs(blocks).max(-1, keepdims=True)
    byte = np.maximum(np.where(amax > 0, np.frexp(amax)[1] - 1 + 127, 0) - down, 1)
    scale = np.exp2(byte - 127.0)
    codes = (blocks / scale).astype(np.float32).astype(dtype).astype(np.float64)
    return np.moveaxis((codes * scale).reshape(v.shape), -1, axis)


WIDE = False


def mx_kscale(k):
    if not WIDE:
        return np.ones(k)
    levels = np.array([10, -10, 5, -5, 0])
    if k % 512:
        return np.exp2(np.random.permutation(np.resize(levels, k // 32))).repeat(32)
    a = np.empty((k // 512, 16))
    for p in range(k // 512):
        a[p, :8] = np.random.permutation(np.resize(levels, 8))
        for g in range(8):
            far = levels[np.abs(levels - a[p, g]) >= 10]
            a[p, g + 8] = far[np.random.randint(len(far))]
    return np.exp2(a.ravel()).repeat(32)


def f64(x):
    return np.asarray(x).astype(np.float64)


def striped(idx):
    return np.tile(idx.reshape(-1, 16).T, (8, 1)).astype(np.uint16)


def unstriped(offs):
    return offs[:16].T.reshape(-1).astype(np.int64)


def striped8(idx):
    return np.concatenate([x.reshape(-1, 16).T for x in idx]).astype(np.uint16)


def runs(offs, k):
    lists = np.stack([offs[16 * r : 16 * r + 16].T.reshape(-1) for r in range(8)]).astype(np.int64)
    return lists[np.arange(k) % 512 // 64]


def pack_weight(w):
    k, n = w.shape
    w = f64(np.asarray(w, np.float32).astype(ml_dtypes.bfloat16)).reshape(k // 32, 32, n)
    amax = np.abs(w).max(1)
    byte = np.clip(np.where(amax > 0, np.frexp(amax)[1] - 1 + 127 - 7, 1), 1, 254)
    scaled = (w * np.exp2(127.0 - byte)[:, None, :]).reshape(k, n).astype(np.float32)
    words = np.ascontiguousarray(scaled.reshape(k // 512, 128, 4, n).transpose(0, 1, 3, 2)).astype(ml_dtypes.float8_e4m3fn).view(np.uint8)
    return words, np.ascontiguousarray(byte.astype(np.uint8).reshape(k // 512, 16, n))


def unpack_weight(words, scales):
    g, p, n, _ = words.shape
    vals = np.ascontiguousarray(words).view(ml_dtypes.float8_e4m3fn).astype(np.float64) * np.repeat(np.exp2(scales.astype(np.float64) - 127.0), 8, axis=1)[..., None]
    return vals.transpose(0, 1, 3, 2).reshape(g * 512, n)

def planes(y):
    n, m = y.shape
    v = y.astype(np.float32).astype(ml_dtypes.bfloat16).astype(np.float64).reshape(n // 32, 32, m)
    top = np.abs(v).max(1)
    byte = np.clip(np.where(top > 0, np.frexp(top)[1] - 1 + 127 - 7, 1), 1, 254)
    codes = (v * np.exp2(127.0 - byte)[:, None, :]).reshape(n, m).astype(np.float32).astype(ml_dtypes.float8_e4m3fn).view(np.uint8)
    words = codes.reshape(n // 512, 128, 4, m).transpose(0, 1, 3, 2)
    return np.ascontiguousarray(words), np.ascontiguousarray(byte.astype(np.uint8).reshape(n // 512, 16, m))


K, T, S, V, G, H, C = 512, 2048, 1024, 512, 2048, 512, 512


def setup_inputs():
    n = np.random.standard_normal
    s = mx_kscale(K)[:, None]
    packed_xT = pack_weight(n((K, T)) * s)
    packed_dT = pack_weight(n((K, G)) / s)
    return {
        "x_words": packed_xT[0],
        "x_scales": packed_xT[1],
        "d_words": packed_dT[0],
        "d_scales": packed_dT[1],
        "gs": (np.random.uniform(0.5, 1.5, (K, 1)) / s).astype(np.float32),
        "offs": striped(np.random.permutation(T)[:S]),
        "k1": striped8(np.random.randint(0, G, (8, H))),
        "n1": striped8(np.stack([np.random.permutation(S) for _ in range(8)])),
        "cand": striped(np.random.permutation(T)[:C]),
        "n2": striped8(np.stack([np.random.permutation(V) for _ in range(8)])),
        "n3": striped8(np.stack([np.random.permutation(V) for _ in range(8)])),
    }


def reference(x_words, x_scales, d_words, d_scales, gs, offs, k1, n1, cand, n2, n3):
    x_cand = unpack_weight(x_words, x_scales)[:, unstriped(cand)]
    d_k1 = unpack_weight(d_words, d_scales)[np.arange(K)[:, None], runs(k1, K)]
    xq = unpack_weight(x_words, x_scales)[:, unstriped(offs)]
    h = 0.0625 * (d_k1.T @ xq)
    ln = h[np.arange(H)[:, None], runs(n1, H)]
    sq = (ln) ** 2
    ms = sq.reshape(H, V, 2).sum(axis=2)
    z = f64(gs) * np.sqrt(ms + 0.1)
    s = 0.0625 * ((x_cand.T @ mxq(z, 0, "e4m3")))
    out_0 = 0.75 * ((s - (s[np.arange(C)[:, None], runs(n2, C)])) * (s - (s[np.arange(C)[:, None], runs(n3, C)])))
    return (out_0,) + planes(out_0)

@@ -1,0 +1,210 @@
+from contextlib import ExitStack
+
+import concourse.mybir as mybir
+
+K, T, S, V, G, H, C = 512, 2048, 1024, 512, 2048, 512, 512
+FLOPS = 2 * K * H * S + 2 * K * C * V
+
+F32 = mybir.dt.float32
+BF16 = mybir.dt.bfloat16
+I32 = mybir.dt.int32
+U32 = mybir.dt.uint32
+U16 = mybir.dt.uint16
+U8 = mybir.dt.uint8
+FP8X4 = mybir.dt.float8_e4m3fn_x4
+ACT = mybir.ActivationFunctionType
+ALU = mybir.AluOpType
+
+P = 128
+PACK = 4
+BANK = 512
+Z_CHUNKS = (128, 128, 128, 128)
+Y_CHUNKS = (256, 128, 128)
+
+
+def spans(widths):
+    starts = [sum(widths[:i]) for i in range(len(widths))]
+    return [(a, a + w) for a, w in zip(starts, widths)]
+
+
+def entries(offsets, first, last):
+    return offsets[:, first // 16 : last // 16]
+
+
+def tile_picked_pqcprmsquad_none_po_kernel(
+    tc, x_words, x_scales, d_words, d_scales, gs, offs, k1, n1, cand, n2, n3, out_0, out_1, out_2
+):
+    nc = tc.nc
+    with ExitStack() as ctx:
+        lists = ctx.enter_context(tc.tile_pool(name="lists", bufs=1))
+        keep = ctx.enter_context(tc.tile_pool(name="keep", bufs=1))
+        psum_h = ctx.enter_context(tc.psum_pool(name="psum_h", bufs=4))
+        psum_s = ctx.enter_context(tc.psum_pool(name="psum_s", bufs=2))
+
+        def load_list(source, name):
+            tile = lists.tile(list(source.shape), U16, name=name)
+            nc.sync.dma_start(tile[:], source)
+            return tile
+
+        d_byte_win = keep.tile([P, G], U8, align_bytes=64)
+        x_byte_win = keep.tile([P, T], U8, align_bytes=64)
+        d_word_win = keep.tile([P, G], I32, align_bytes=64)
+        x_word_win = keep.tile([P, T], I32, align_bytes=64)
+        gain = keep.tile([P, PACK], F32)
+
+        k1_t = load_list(k1, "k1_t")
+        nc.sync.dma_start(
+            d_byte_win[:].bitcast(I32),
+            d_scales[0].bitcast(I32).unsqueeze(1).broadcast_to([16, 8, G // 4]),
+        )
+        offs_t = load_list(offs, "offs_t")
+        for q in range(4):
+            nc.scalar.dma_start(
+                x_byte_win[32 * q : 32 * q + 32, :].bitcast(I32),
+                x_scales[0, 4 * q : 4 * q + 4, :].bitcast(I32).unsqueeze(0).broadcast_to([8, 4, T // 4]),
+            )
+        nc.sync.dma_start(d_word_win[:], d_words[0].rearrange("p n t -> p (n t)").bitcast(I32))
+        nc.sync.dma_start(x_word_win[:], x_words[0].rearrange("p n t -> p (n t)").bitcast(I32))
+        cand_t = load_list(cand, "cand_t")
+        n1_t = load_list(n1, "n1_t")
+        nc.sync.dma_start(gain[:], gs.rearrange("(p t) o -> p (t o)", t=PACK))
+        n2_t = load_list(n2, "n2_t")
+        n3_t = load_list(n3, "n3_t")
+
+        warm_in = keep.tile([P, 1], F32)
+        warm_out = keep.tile([P, 1], F32)
+        nc.gpsimd.memset(warm_in[:], 1.0)
+        nc.scalar.activation(warm_out[:], warm_in[:], ACT.Sqrt)
+
+        def deal(dealt, picked):
+            nc.vector.tensor_copy(
+                dealt[:].rearrange("p (t m) -> p t m", t=PACK),
+                picked[:].rearrange("p (m t) -> p t m", t=PACK),
+            )
+
+        d_bytes_picked = keep.tile([P, H], U8, align_bytes=64)
+        d_bytes_dealt = keep.tile([P, H], U8, align_bytes=64)
+        d_plane = keep.tile([P, H], U8, align_bytes=64)
+        nc.gpsimd.memset(d_plane[:].bitcast(I32), 0)
+        nc.vector.tensor_copy(d_bytes_picked[:], d_byte_win[:].indirect(k1_t[:]))
+        deal(d_bytes_dealt, d_bytes_picked)
+        for r in range(4):
+            nc.sync.dma_start(d_plane[r:P:32, :].bitcast(I32), d_bytes_dealt[8 * r : P : 32, :].bitcast(I32))
+
+        tok_plane = keep.tile([P, S], U8, align_bytes=64)
+        nc.vector.tensor_copy(tok_plane[:], x_byte_win[:].indirect(offs_t[:]))
+
+        d_words_picked = keep.tile([P, H], U32, align_bytes=64)
+        d_codes = keep.tile([P, H], U32, align_bytes=64)
+        nc.vector.tensor_copy(d_words_picked[:], d_word_win[:].bitcast(U32).indirect(k1_t[:]))
+        deal(d_codes, d_words_picked)
+
+        sq_win = [keep.tile([P, S], F32, name="sq_win%d" % t) for t in range(PACK)]
+        halves = spans((BANK,) * (S // BANK))
+        tok_codes = [keep.tile([P, BANK], U32, align_bytes=64, name="tok_codes%d" % a) for a, b in halves]
+        for codes, (a, b) in zip(tok_codes, halves):
+            nc.vector.tensor_copy(codes[:], x_word_win[:].bitcast(U32).indirect(entries(offs_t, a, b)))
+        for t in range(PACK):
+            rows = slice(t * P, (t + 1) * P)
+            for codes, (a, b) in zip(tok_codes, halves):
+                h_acc = psum_h.tile([P, BANK], F32, name="h_acc")
+                nc.tensor.matmul_mx(
+                    out=h_acc[:],
+                    lhsT=d_codes[:, rows].bitcast(FP8X4),
+                    lhsT_scale=d_plane[:, rows],
+                    rhs=codes[:].bitcast(FP8X4),
+                    rhs_scale=tok_plane[:, a:b],
+                    start=True,
+                    stop=True,
+                )
+                nc.scalar.activation(sq_win[t][:, a:b], h_acc[:], ACT.Square, scale=0.0625)
+
+        c_words_picked = keep.tile([P, C], U32, align_bytes=64)
+        c_codes = keep.tile([P, C], U32, align_bytes=64)
+        nc.vector.tensor_copy(c_words_picked[:], x_word_win[:].bitcast(U32).indirect(cand_t[:]))
+        deal(c_codes, c_words_picked)
+
+        z_codes = keep.tile([P, V], U32, align_bytes=64)
+        z_plane = keep.tile([P, V], U8, align_bytes=64)
+        z_spans = spans(Z_CHUNKS)
+        for c, (v0, v1) in enumerate(z_spans):
+            w = v1 - v0
+            lined = keep.tile([P, PACK, 2 * w], F32, name="lined", tag="lined%d" % (c % 2), align_bytes=64)
+            for t in range(PACK):
+                nc.vector.tensor_copy(lined[:, t, :], sq_win[t][:].indirect(entries(n1_t, 2 * v0, 2 * v1)))
+            pairs = lined[:].rearrange("p t (v e) -> p (t v) e", e=2)
+            ms = keep.tile([P, PACK * w], F32, name="ms%d" % c)
+            nc.vector.tensor_tensor(ms[:], pairs[:, :, 0], pairs[:, :, 1], ALU.add)
+            root = keep.tile([P, PACK, w], F32, name="root%d" % c)
+            nc.scalar.activation(root[:].rearrange("p t v -> p (t v)"), ms[:], ACT.Sqrt, bias=0.1)
+            z_rows = keep.tile([P, PACK, w], BF16, name="z_rows%d" % c)
+            for t in range(PACK):
+                nc.scalar.activation(z_rows[:, t, :], root[:, t, :], ACT.Copy, scale=gain[:, t : t + 1])
+            z_woven = keep.tile([P, w, PACK], BF16, align_bytes=64, name="z_woven%d" % c)
+            nc.scalar.copy(z_woven[:], z_rows[:].rearrange("p t v -> p v t"))
+            nc.vector.quantize_mx(
+                out=z_codes[:, v0:v1].bitcast(FP8X4),
+                scales=z_plane[:, v0:v1],
+                in_=z_woven[:].rearrange("p v t -> p (v t)"),
+            )
+
+        c_bytes_picked = keep.tile([P, C], U8, tag="lined%d" % ((len(z_spans) - 1) % 2), align_bytes=64)
+        c_plane = keep.tile([P, C], U8, align_bytes=64)
+        nc.vector.tensor_copy(c_bytes_picked[:], x_byte_win[:].indirect(cand_t[:]))
+        deal(c_plane, c_bytes_picked)
+
+        s_win = [keep.tile([P, V], F32, name="s_win%d" % t) for t in range(PACK)]
+        s_own = [keep.tile([P, V], F32, name="s_own%d" % t) for t in range(PACK)]
+        last = z_spans[-1][0]
+        for t in range(PACK):
+            rows = slice(t * P, (t + 1) * P)
+            for part, pieces in enumerate((spans((256, 128)), [(last, V)])):
+                s_acc = psum_s.tile([P, V], F32, name="s_acc", tag="s_acc%d" % part)
+                for v0, v1 in pieces:
+                    nc.tensor.matmul_mx(
+                        out=s_acc[:, v0:v1],
+                        lhsT=c_codes[:, rows].bitcast(FP8X4),
+                        lhsT_scale=c_plane[:, rows],
+                        rhs=z_codes[:, v0:v1].bitcast(FP8X4),
+                        rhs_scale=z_plane[:, v0:v1],
+                        start=True,
+                        stop=True,
+                    )
+                cols = slice(pieces[0][0], pieces[-1][1])
+                nc.scalar.activation(s_win[t][:, cols], s_acc[:, cols], ACT.Copy, scale=0.0625)
+                nc.scalar.activation(s_own[t][:, cols], s_acc[:, cols], ACT.Copy, scale=0.0625)
+
+        out_rows = out_0.rearrange("(p t) v -> p t v", t=PACK)
+        out_words = out_1[0].rearrange("p v t -> p (v t)").bitcast(I32)
+        y_codes = keep.tile([P, V], I32, align_bytes=64)
+        y_plane = keep.tile([P, V], U8, align_bytes=64)
+        for c, (v0, v1) in enumerate(spans(Y_CHUNKS)):
+            w = v1 - v0
+            diff2 = keep.tile([P, PACK, w], F32, name="diff2", tag="diff2_%d" % (c % 2))
+            diff3 = keep.tile([P, PACK, w], F32, name="diff3", tag="diff3_%d" % (c % 2))
+            for t in range(PACK):
+                for diff, pos in ((diff2, n2_t), (diff3, n3_t)):
+                    nc.vector.tensor_tensor(
+                        diff[:, t, :], s_win[t][:].indirect(entries(pos, v0, v1)), s_own[t][:, v0:v1], ALU.subtract
+                    )
+            y = keep.tile([P, PACK, w], F32, name="y%d" % c)
+            nc.vector.scalar_tensor_tensor(
+                y[:].rearrange("p t v -> p (t v)"),
+                diff2[:].rearrange("p t v -> p (t v)"),
+                0.75,
+                diff3[:].rearrange("p t v -> p (t v)"),
+                ALU.mult,
+                ALU.mult,
+            )
+            nc.sync.dma_start(out_rows[:, :, v0:v1], y[:])
+            y_woven = keep.tile([P, w, PACK], BF16, align_bytes=64, name="y_woven%d" % c)
+            nc.scalar.copy(y_woven[:], y[:].rearrange("p t v -> p v t"))
+            nc.vector.quantize_mx(
+                out=y_codes[:, v0:v1].bitcast(FP8X4),
+                scales=y_plane[:, v0:v1],
+                in_=y_woven[:].rearrange("p v t -> p (v t)"),
+            )
+            nc.sync.dma_start(out_words[:, v0:v1], y_codes[:, v0:v1])
+        for q in range(4):
+            queue = nc.sync if q % 2 else nc.scalar
+            queue.dma_start(out_2[0, 4 * q : 4 * q + 4, :].bitcast(I32), y_plane[32 * q : 32 * q + 4, :].bitcast(I32))

@@ -18,7 +18,7 @@ ALU = mybir.AluOpType
 P = 128
 PACK = 4
 BANK = 512
-Z_CHUNKS = (128, 128, 128, 128)
+Z_CHUNKS = (256, 128, 128)
 Y_CHUNKS = (256, 128, 128)
 
 
@@ -38,8 +38,9 @@ def tile_picked_pqcprmsquad_none_po_kernel(
     with ExitStack() as ctx:
         lists = ctx.enter_context(tc.tile_pool(name="lists", bufs=1))
         keep = ctx.enter_context(tc.tile_pool(name="keep", bufs=1))
+        ring = ctx.enter_context(tc.tile_pool(name="ring", bufs=1))
         psum_h = ctx.enter_context(tc.psum_pool(name="psum_h", bufs=4))
-        psum_s = ctx.enter_context(tc.psum_pool(name="psum_s", bufs=2))
+        psum_s = ctx.enter_context(tc.psum_pool(name="psum_s", bufs=4))
 
         def load_list(source, name):
             tile = lists.tile(list(source.shape), U16, name=name)
@@ -59,21 +60,21 @@ def tile_picked_pqcprmsquad_none_po_kernel(
         )
         offs_t = load_list(offs, "offs_t")
         for q in range(4):
-            nc.scalar.dma_start(
+            nc.sync.dma_start(
                 x_byte_win[32 * q : 32 * q + 32, :].bitcast(I32),
                 x_scales[0, 4 * q : 4 * q + 4, :].bitcast(I32).unsqueeze(0).broadcast_to([8, 4, T // 4]),
             )
         nc.sync.dma_start(d_word_win[:], d_words[0].rearrange("p n t -> p (n t)").bitcast(I32))
-        nc.sync.dma_start(x_word_win[:], x_words[0].rearrange("p n t -> p (n t)").bitcast(I32))
         cand_t = load_list(cand, "cand_t")
         n1_t = load_list(n1, "n1_t")
+        nc.sync.dma_start(x_word_win[:], x_words[0].rearrange("p n t -> p (n t)").bitcast(I32))
         nc.sync.dma_start(gain[:], gs.rearrange("(p t) o -> p (t o)", t=PACK))
         n2_t = load_list(n2, "n2_t")
         n3_t = load_list(n3, "n3_t")
 
         warm_in = keep.tile([P, 1], F32)
         warm_out = keep.tile([P, 1], F32)
-        nc.gpsimd.memset(warm_in[:], 1.0)
+        nc.vector.memset(warm_in[:], 1.0)
         nc.scalar.activation(warm_out[:], warm_in[:], ACT.Sqrt)
 
         def deal(dealt, picked):
@@ -85,7 +86,7 @@ def tile_picked_pqcprmsquad_none_po_kernel(
         d_bytes_picked = keep.tile([P, H], U8, align_bytes=64)
         d_bytes_dealt = keep.tile([P, H], U8, align_bytes=64)
         d_plane = keep.tile([P, H], U8, align_bytes=64)
-        nc.gpsimd.memset(d_plane[:].bitcast(I32), 0)
+        nc.vector.memset(d_plane[:].bitcast(I32), 0)
         nc.vector.tensor_copy(d_bytes_picked[:], d_byte_win[:].indirect(k1_t[:]))
         deal(d_bytes_dealt, d_bytes_picked)
         for r in range(4):
@@ -124,42 +125,56 @@ def tile_picked_pqcprmsquad_none_po_kernel(
         nc.vector.tensor_copy(c_words_picked[:], x_word_win[:].bitcast(U32).indirect(cand_t[:]))
         deal(c_codes, c_words_picked)
 
+        z_rows = ring.tile([P, PACK, V], BF16, offset=0)
         z_codes = keep.tile([P, V], U32, align_bytes=64)
         z_plane = keep.tile([P, V], U8, align_bytes=64)
-        z_spans = spans(Z_CHUNKS)
-        for c, (v0, v1) in enumerate(z_spans):
-            w = v1 - v0
-            lined = keep.tile([P, PACK, 2 * w], F32, name="lined", tag="lined%d" % (c % 2), align_bytes=64)
-            for t in range(PACK):
-                nc.vector.tensor_copy(lined[:, t, :], sq_win[t][:].indirect(entries(n1_t, 2 * v0, 2 * v1)))
-            pairs = lined[:].rearrange("p t (v e) -> p (t v) e", e=2)
-            ms = keep.tile([P, PACK * w], F32, name="ms%d" % c)
-            nc.vector.tensor_tensor(ms[:], pairs[:, :, 0], pairs[:, :, 1], ALU.add)
-            root = keep.tile([P, PACK, w], F32, name="root%d" % c)
-            nc.scalar.activation(root[:].rearrange("p t v -> p (t v)"), ms[:], ACT.Sqrt, bias=0.1)
-            z_rows = keep.tile([P, PACK, w], BF16, name="z_rows%d" % c)
-            for t in range(PACK):
-                nc.scalar.activation(z_rows[:, t, :], root[:, t, :], ACT.Copy, scale=gain[:, t : t + 1])
-            z_woven = keep.tile([P, w, PACK], BF16, align_bytes=64, name="z_woven%d" % c)
-            nc.scalar.copy(z_woven[:], z_rows[:].rearrange("p t v -> p v t"))
-            nc.vector.quantize_mx(
-                out=z_codes[:, v0:v1].bitcast(FP8X4),
-                scales=z_plane[:, v0:v1],
-                in_=z_woven[:].rearrange("p v t -> p (v t)"),
-            )
+        for t in range(PACK):
+            final = t == PACK - 1
+            for v0, v1 in spans(Z_CHUNKS if final else (V // 2, V // 2)):
+                w = v1 - v0
+                if final and v1 == V:
+                    lined = ring.tile([P, 2 * w], F32, name="lined_last", offset=8192)
+                else:
+                    lined = keep.tile([P, 2 * w], F32, name="lined%d_%d" % (t, v0))
+                nc.vector.tensor_copy(lined[:], sq_win[t][:].indirect(entries(n1_t, 2 * v0, 2 * v1)))
+                pairs = lined[:].rearrange("p (v e) -> p v e", e=2)
+                ms = keep.tile([P, w], F32, name="ms%d_%d" % (t, v0))
+                nc.vector.tensor_tensor(ms[:], pairs[:, :, 0], pairs[:, :, 1], ALU.add)
+                root = keep.tile([P, w], F32, name="root%d_%d" % (t, v0))
+                nc.scalar.activation(root[:], ms[:], ACT.Sqrt, bias=0.1)
+                nc.scalar.activation(z_rows[:, t, v0:v1], root[:], ACT.Copy, scale=gain[:, t : t + 1])
+                if final:
+                    z_woven = keep.tile([P, w, PACK], BF16, align_bytes=64, name="z_woven%d" % v0)
+                    nc.scalar.copy(z_woven[:], z_rows[:, :, v0:v1].rearrange("p t v -> p v t"))
+                    nc.vector.quantize_mx(
+                        out=z_codes[:, v0:v1].bitcast(FP8X4),
+                        scales=z_plane[:, v0:v1],
+                        in_=z_woven[:].rearrange("p v t -> p (v t)"),
+                    )
 
-        c_bytes_picked = keep.tile([P, C], U8, tag="lined%d" % ((len(z_spans) - 1) % 2), align_bytes=64)
+        c_bytes_picked = ring.tile([P, C], U8, offset=8192)
         c_plane = keep.tile([P, C], U8, align_bytes=64)
         nc.vector.tensor_copy(c_bytes_picked[:], x_byte_win[:].indirect(cand_t[:]))
         deal(c_plane, c_bytes_picked)
 
-        s_win = [keep.tile([P, V], F32, name="s_win%d" % t) for t in range(PACK)]
-        s_own = [keep.tile([P, V], F32, name="s_own%d" % t) for t in range(PACK)]
-        last = z_spans[-1][0]
+        out_rows = out_0.rearrange("(p t) v -> p t v", t=PACK)
+        out_words = out_1[0].rearrange("p v t -> p (v t)").bitcast(I32)
+        y = keep.tile([P, PACK, V], F32)
+        y_codes = keep.tile([P, V], I32, align_bytes=64)
+        y_plane = keep.tile([P, V], U8, align_bytes=64)
+        z_spans = spans(Z_CHUNKS)
+        s_win, s_own = [], []
         for t in range(PACK):
             rows = slice(t * P, (t + 1) * P)
-            for part, pieces in enumerate((spans((256, 128)), [(last, V)])):
-                s_acc = psum_s.tile([P, V], F32, name="s_acc", tag="s_acc%d" % part)
+            width = V if t == PACK - 1 else 2 * V
+            if t == 0:
+                s_own.append(ring.tile([P, V], F32, name="s_own0", offset=0))
+                s_win.append(ring.tile([P, width], F32, name="s_win0", offset=2048))
+            else:
+                s_own.append(keep.tile([P, V], F32, name="s_own%d" % t))
+                s_win.append(keep.tile([P, width], F32, name="s_win%d" % t))
+            for pieces in (z_spans[:-1], z_spans[-1:]) if t == 0 else ([(0, V)],):
+                s_acc = psum_s.tile([P, V], F32, name="s_acc")
                 for v0, v1 in pieces:
                     nc.tensor.matmul_mx(
                         out=s_acc[:, v0:v1],
@@ -174,37 +189,38 @@ def tile_picked_pqcprmsquad_none_po_kernel(
                 nc.scalar.activation(s_win[t][:, cols], s_acc[:, cols], ACT.Copy, scale=0.0625)
                 nc.scalar.activation(s_own[t][:, cols], s_acc[:, cols], ACT.Copy, scale=0.0625)
 
-        out_rows = out_0.rearrange("(p t) v -> p t v", t=PACK)
-        out_words = out_1[0].rearrange("p v t -> p (v t)").bitcast(I32)
-        y_codes = keep.tile([P, V], I32, align_bytes=64)
-        y_plane = keep.tile([P, V], U8, align_bytes=64)
-        for c, (v0, v1) in enumerate(spans(Y_CHUNKS)):
-            w = v1 - v0
-            diff2 = keep.tile([P, PACK, w], F32, name="diff2", tag="diff2_%d" % (c % 2))
-            diff3 = keep.tile([P, PACK, w], F32, name="diff3", tag="diff3_%d" % (c % 2))
-            for t in range(PACK):
-                for diff, pos in ((diff2, n2_t), (diff3, n3_t)):
-                    nc.vector.tensor_tensor(
-                        diff[:, t, :], s_win[t][:].indirect(entries(pos, v0, v1)), s_own[t][:, v0:v1], ALU.subtract
-                    )
-            y = keep.tile([P, PACK, w], F32, name="y%d" % c)
-            nc.vector.scalar_tensor_tensor(
-                y[:].rearrange("p t v -> p (t v)"),
-                diff2[:].rearrange("p t v -> p (t v)"),
-                0.75,
-                diff3[:].rearrange("p t v -> p (t v)"),
-                ALU.mult,
-                ALU.mult,
-            )
-            nc.sync.dma_start(out_rows[:, :, v0:v1], y[:])
-            y_woven = keep.tile([P, w, PACK], BF16, align_bytes=64, name="y_woven%d" % c)
-            nc.scalar.copy(y_woven[:], y[:].rearrange("p t v -> p v t"))
-            nc.vector.quantize_mx(
-                out=y_codes[:, v0:v1].bitcast(FP8X4),
-                scales=y_plane[:, v0:v1],
-                in_=y_woven[:].rearrange("p v t -> p (v t)"),
-            )
-            nc.sync.dma_start(out_words[:, v0:v1], y_codes[:, v0:v1])
+        def differences(t, v0, v1):
+            made = []
+            for pos, name in ((n2_t, "diff2"), (n3_t, "diff3")):
+                diff = keep.tile([P, v1 - v0], F32, name="%s_%d_%d" % (name, t, v0))
+                nc.vector.tensor_tensor(
+                    diff[:], s_win[t][:].indirect(entries(pos, v0, v1)), s_own[t][:, v0:v1], ALU.subtract
+                )
+                made.append(diff)
+            return made
+
+        def finish(t, v0, v1, diff2, diff3):
+            nc.vector.scalar_tensor_tensor(y[:, t, v0:v1], diff2[:], 0.75, diff3[:], ALU.mult, ALU.mult)
+            nc.sync.dma_start(out_rows[:, t, v0:v1], y[:, t, v0:v1])
+            if t == PACK - 1:
+                y_woven = keep.tile([P, v1 - v0, PACK], BF16, align_bytes=64, name="y_woven%d" % v0)
+                weave = nc.vector.tensor_copy if v1 == V else nc.scalar.copy
+                weave(y_woven[:], y[:, :, v0:v1].rearrange("p t v -> p v t"))
+                nc.vector.quantize_mx(
+                    out=y_codes[:, v0:v1].bitcast(FP8X4),
+                    scales=y_plane[:, v0:v1],
+                    in_=y_woven[:].rearrange("p v t -> p (v t)"),
+                )
+                nc.sync.dma_start(out_words[:, v0:v1], y_codes[:, v0:v1])
+
+        steps = [(t, 0, V) for t in range(PACK - 1)] + [(PACK - 1, v0, v1) for v0, v1 in spans(Y_CHUNKS)]
+        pending = None
+        for step in steps:
+            diffs = differences(*step)
+            if pending:
+                finish(*pending)
+            pending = (*step, *diffs)
+        finish(*pending)
         for q in range(4):
             queue = nc.sync if q % 2 else nc.scalar
             queue.dma_start(out_2[0, 4 * q : 4 * q + 4, :].bitcast(I32), y_plane[32 * q : 32 * q + 4, :].bitcast(I32))

@@ -1,3 +1,4 @@
+import math
 from contextlib import ExitStack
 
 import concourse.mybir as mybir
@@ -15,6 +16,7 @@ FP8X4 = mybir.dt.float8_e4m3fn_x4
 ACT = mybir.ActivationFunctionType
 ALU = mybir.AluOpType
 
+S_SCALE = 0.0625 * math.sqrt(0.75)
 P = 128
 PACK = 4
 BANK = 512
@@ -40,7 +42,7 @@ def tile_picked_pqcprmsquad_none_po_kernel(
         keep = ctx.enter_context(tc.tile_pool(name="keep", bufs=1))
         ring = ctx.enter_context(tc.tile_pool(name="ring", bufs=1))
         psum_h = ctx.enter_context(tc.psum_pool(name="psum_h", bufs=4))
-        psum_s = ctx.enter_context(tc.psum_pool(name="psum_s", bufs=4))
+        psum_s = ctx.enter_context(tc.psum_pool(name="psum_s", bufs=3))
 
         def load_list(source, name):
             tile = lists.tile(list(source.shape), U16, name=name)
@@ -100,7 +102,7 @@ def tile_picked_pqcprmsquad_none_po_kernel(
         nc.vector.tensor_copy(d_words_picked[:], d_word_win[:].bitcast(U32).indirect(k1_t[:]))
         deal(d_codes, d_words_picked)
 
-        sq_win = [keep.tile([P, S], F32, name="sq_win%d" % t) for t in range(PACK)]
+        sq_win = [keep.tile([P, S if t == PACK - 1 else 2 * S], F32, name="sq_win%d" % t) for t in range(PACK)]
         halves = spans((BANK,) * (S // BANK))
         tok_codes = [keep.tile([P, BANK], U32, align_bytes=64, name="tok_codes%d" % a) for a, b in halves]
         for codes, (a, b) in zip(tok_codes, halves):
@@ -130,7 +132,7 @@ def tile_picked_pqcprmsquad_none_po_kernel(
         z_plane = keep.tile([P, V], U8, align_bytes=64)
         for t in range(PACK):
             final = t == PACK - 1
-            for v0, v1 in spans(Z_CHUNKS if final else (V // 2, V // 2)):
+            for v0, v1 in spans(Z_CHUNKS if final else (V,)):
                 w = v1 - v0
                 if final and v1 == V:
                     lined = ring.tile([P, 2 * w], F32, name="lined_last", offset=8192)
@@ -139,7 +141,7 @@ def tile_picked_pqcprmsquad_none_po_kernel(
                 nc.vector.tensor_copy(lined[:], sq_win[t][:].indirect(entries(n1_t, 2 * v0, 2 * v1)))
                 pairs = lined[:].rearrange("p (v e) -> p v e", e=2)
                 ms = keep.tile([P, w], F32, name="ms%d_%d" % (t, v0))
-                nc.vector.tensor_tensor(ms[:], pairs[:, :, 0], pairs[:, :, 1], ALU.add)
+                (nc.vector if final else nc.gpsimd).tensor_tensor(ms[:], pairs[:, :, 0], pairs[:, :, 1], ALU.add)
                 root = keep.tile([P, w], F32, name="root%d_%d" % (t, v0))
                 nc.scalar.activation(root[:], ms[:], ACT.Sqrt, bias=0.1)
                 nc.scalar.activation(z_rows[:, t, v0:v1], root[:], ACT.Copy, scale=gain[:, t : t + 1])
@@ -163,21 +165,22 @@ def tile_picked_pqcprmsquad_none_po_kernel(
         y_codes = keep.tile([P, V], I32, align_bytes=64)
         y_plane = keep.tile([P, V], U8, align_bytes=64)
         z_spans = spans(Z_CHUNKS)
-        s_win, s_own = [], []
+        s_win, s_acc = [], []
         for t in range(PACK):
             rows = slice(t * P, (t + 1) * P)
             width = V if t == PACK - 1 else 2 * V
             if t == 0:
-                s_own.append(ring.tile([P, V], F32, name="s_own0", offset=0))
-                s_win.append(ring.tile([P, width], F32, name="s_win0", offset=2048))
+                s_win.append(ring.tile([P, width], F32, name="s_win0", offset=0))
             else:
-                s_own.append(keep.tile([P, V], F32, name="s_own%d" % t))
                 s_win.append(keep.tile([P, width], F32, name="s_win%d" % t))
+            s_acc.append([])
             for pieces in (z_spans[:-1], z_spans[-1:]) if t == 0 else ([(0, V)],):
-                s_acc = psum_s.tile([P, V], F32, name="s_acc")
+                first, last = pieces[0][0], pieces[-1][1]
+                pool = psum_h if t == 0 else psum_s
+                bank = pool.tile([P, BANK], F32, name="h_acc" if t == 0 else "s_acc")
                 for v0, v1 in pieces:
                     nc.tensor.matmul_mx(
-                        out=s_acc[:, v0:v1],
+                        out=bank[:, v0:v1],
                         lhsT=c_codes[:, rows].bitcast(FP8X4),
                         lhsT_scale=c_plane[:, rows],
                         rhs=z_codes[:, v0:v1].bitcast(FP8X4),
@@ -185,22 +188,33 @@ def tile_picked_pqcprmsquad_none_po_kernel(
                         start=True,
                         stop=True,
                     )
-                cols = slice(pieces[0][0], pieces[-1][1])
-                nc.scalar.activation(s_win[t][:, cols], s_acc[:, cols], ACT.Copy, scale=0.0625)
-                nc.scalar.activation(s_own[t][:, cols], s_acc[:, cols], ACT.Copy, scale=0.0625)
+                nc.scalar.activation(s_win[t][:, first:last], bank[:, first:last], ACT.Copy, scale=S_SCALE)
+                s_acc[t].append((bank, first, last))
+
+        def less(diff, fetched, t, v0, v1):
+            for bank, first, last in s_acc[t]:
+                a, b = max(first, v0), min(last, v1)
+                nc.vector.scalar_tensor_tensor(
+                    diff[:, a - v0 : b - v0], bank[:, a:b], S_SCALE, fetched[:, a - v0 : b - v0], ALU.mult, ALU.subtract
+                )
 
         def differences(t, v0, v1):
-            made = []
-            for pos, name in ((n2_t, "diff2"), (n3_t, "diff3")):
-                diff = keep.tile([P, v1 - v0], F32, name="%s_%d_%d" % (name, t, v0))
-                nc.vector.tensor_tensor(
-                    diff[:], s_win[t][:].indirect(entries(pos, v0, v1)), s_own[t][:, v0:v1], ALU.subtract
-                )
-                made.append(diff)
-            return made
+            at2, at3, diff2, diff3 = [
+                keep.tile([P, v1 - v0], F32, name="%s_%d_%d" % (name, t, v0)) for name in ("at2", "at3", "diff2", "diff3")
+            ]
+            nc.vector.tensor_copy(at3[:], s_win[t][:].indirect(entries(n3_t, v0, v1)))
+            nc.vector.tensor_copy(at2[:], s_win[t][:].indirect(entries(n2_t, v0, v1)))
+            if t == PACK - 1:
+                less(diff3, at3, t, v0, v1)
+                less(diff2, at2, t, v0, v1)
+            else:
+                less(diff3, at3, t, v0, v1)
+                nc.gpsimd.tensor_tensor(diff2[:], s_win[t][:, v0:v1], at2[:], ALU.subtract)
+            return diff2, diff3
 
         def finish(t, v0, v1, diff2, diff3):
-            nc.vector.scalar_tensor_tensor(y[:, t, v0:v1], diff2[:], 0.75, diff3[:], ALU.mult, ALU.mult)
+            engine = nc.vector if t == PACK - 1 else nc.gpsimd
+            engine.tensor_tensor(y[:, t, v0:v1], diff2[:], diff3[:], ALU.mult)
             nc.sync.dma_start(out_rows[:, t, v0:v1], y[:, t, v0:v1])
             if t == PACK - 1:
                 y_woven = keep.tile([P, v1 - v0, PACK], BF16, align_bytes=64, name="y_woven%d" % v0)

@@ -1,4 +1,3 @@
-import math
 from contextlib import ExitStack
 
 import concourse.mybir as mybir
@@ -16,7 +15,8 @@ FP8X4 = mybir.dt.float8_e4m3fn_x4
 ACT = mybir.ActivationFunctionType
 ALU = mybir.AluOpType
 
-S_SCALE = 0.0625 * math.sqrt(0.75)
+WHOLE = 2
+TAIL = 64
 P = 128
 PACK = 4
 BANK = 512
@@ -74,15 +74,15 @@ def tile_picked_pqcprmsquad_none_po_kernel(
         n2_t = load_list(n2, "n2_t")
         n3_t = load_list(n3, "n3_t")
 
-        warm_in = keep.tile([P, 1], F32)
-        warm_out = keep.tile([P, 1], F32)
-        nc.vector.memset(warm_in[:], 1.0)
-        nc.scalar.activation(warm_out[:], warm_in[:], ACT.Sqrt)
+        s_scale_squared = keep.tile([P, 1], F32)
+        s_scale = keep.tile([P, 1], F32)
+        nc.vector.memset(s_scale_squared[:], 0.75 / 256)
+        nc.scalar.activation(s_scale[:], s_scale_squared[:], ACT.Sqrt)
 
-        def deal(dealt, picked):
+        def deal(dealt, picked, t0=0, t1=PACK):
             nc.vector.tensor_copy(
-                dealt[:].rearrange("p (t m) -> p t m", t=PACK),
-                picked[:].rearrange("p (m t) -> p t m", t=PACK),
+                dealt[:].rearrange("p (t h m) -> p h t m", h=2, m=P // 2),
+                picked[:].rearrange("p (h m t) -> p h t m", h=2, t=PACK)[:, :, t0:t1, :],
             )
 
         d_bytes_picked = keep.tile([P, H], U8, align_bytes=64)
@@ -102,11 +102,12 @@ def tile_picked_pqcprmsquad_none_po_kernel(
         nc.vector.tensor_copy(d_words_picked[:], d_word_win[:].bitcast(U32).indirect(k1_t[:]))
         deal(d_codes, d_words_picked)
 
-        sq_win = [keep.tile([P, S if t == PACK - 1 else 2 * S], F32, name="sq_win%d" % t) for t in range(PACK)]
+        sq_win = [keep.tile([P, S if t >= WHOLE else 2 * S], F32, name="sq_win%d" % t) for t in range(PACK)]
         halves = spans((BANK,) * (S // BANK))
         tok_codes = [keep.tile([P, BANK], U32, align_bytes=64, name="tok_codes%d" % a) for a, b in halves]
         for codes, (a, b) in zip(tok_codes, halves):
             nc.vector.tensor_copy(codes[:], x_word_win[:].bitcast(U32).indirect(entries(offs_t, a, b)))
+        tails = []
         for t in range(PACK):
             rows = slice(t * P, (t + 1) * P)
             for codes, (a, b) in zip(tok_codes, halves):
@@ -120,97 +121,132 @@ def tile_picked_pqcprmsquad_none_po_kernel(
                     start=True,
                     stop=True,
                 )
-                nc.scalar.activation(sq_win[t][:, a:b], h_acc[:], ACT.Square, scale=0.0625)
+                width = BANK - TAIL if t >= WHOLE and b == S else BANK
+                nc.scalar.activation(sq_win[t][:, a : a + width], h_acc[:, :width], ACT.Square, scale=0.0625)
+                if width < BANK:
+                    tails.append((t, h_acc))
+        for t, h_acc in tails:
+            nc.scalar.activation(sq_win[t][:, S - TAIL :], h_acc[:, BANK - TAIL :], ACT.Square, scale=0.0625)
 
         c_words_picked = keep.tile([P, C], U32, align_bytes=64)
-        c_codes = keep.tile([P, C], U32, align_bytes=64)
+        c_codes_first = keep.tile([P, P], U32, align_bytes=64)
         nc.vector.tensor_copy(c_words_picked[:], x_word_win[:].bitcast(U32).indirect(cand_t[:]))
-        deal(c_codes, c_words_picked)
+        deal(c_codes_first, c_words_picked, 0, 1)
 
         z_rows = ring.tile([P, PACK, V], BF16, offset=0)
         z_codes = keep.tile([P, V], U32, align_bytes=64)
         z_plane = keep.tile([P, V], U8, align_bytes=64)
-        for t in range(PACK):
-            final = t == PACK - 1
-            for v0, v1 in spans(Z_CHUNKS if final else (V,)):
-                w = v1 - v0
-                if final and v1 == V:
-                    lined = ring.tile([P, 2 * w], F32, name="lined_last", offset=8192)
-                else:
-                    lined = keep.tile([P, 2 * w], F32, name="lined%d_%d" % (t, v0))
-                nc.vector.tensor_copy(lined[:], sq_win[t][:].indirect(entries(n1_t, 2 * v0, 2 * v1)))
-                pairs = lined[:].rearrange("p (v e) -> p v e", e=2)
-                ms = keep.tile([P, w], F32, name="ms%d_%d" % (t, v0))
-                (nc.vector if final else nc.gpsimd).tensor_tensor(ms[:], pairs[:, :, 0], pairs[:, :, 1], ALU.add)
-                root = keep.tile([P, w], F32, name="root%d_%d" % (t, v0))
-                nc.scalar.activation(root[:], ms[:], ACT.Sqrt, bias=0.1)
-                nc.scalar.activation(z_rows[:, t, v0:v1], root[:], ACT.Copy, scale=gain[:, t : t + 1])
-                if final:
-                    z_woven = keep.tile([P, w, PACK], BF16, align_bytes=64, name="z_woven%d" % v0)
-                    nc.scalar.copy(z_woven[:], z_rows[:, :, v0:v1].rearrange("p t v -> p v t"))
-                    nc.vector.quantize_mx(
-                        out=z_codes[:, v0:v1].bitcast(FP8X4),
-                        scales=z_plane[:, v0:v1],
-                        in_=z_woven[:].rearrange("p v t -> p (v t)"),
-                    )
+        def line_up(tiles, v0, v1):
+            w, last = v1 - v0, v1 == V and tiles[-1] == PACK - 1
+            name = "%d_%d" % (tiles[0], v0)
+            if last:
+                lined = ring.tile([P, len(tiles), 2 * w], F32, name="lined_last", offset=8192)
+            else:
+                lined = keep.tile([P, len(tiles), 2 * w], F32, name="lined" + name)
+            for i, t in enumerate(tiles):
+                nc.vector.tensor_copy(lined[:, i, :], sq_win[t][:].indirect(entries(n1_t, 2 * v0, 2 * v1)))
+            pairs = lined[:].rearrange("p t (v e) -> p (t v) e", e=2)
+            ms = keep.tile([P, len(tiles) * w], F32, name="ms" + name)
+            (nc.vector if last else nc.gpsimd).tensor_tensor(ms[:], pairs[:, :, 0], pairs[:, :, 1], ALU.add)
+            root = keep.tile([P, len(tiles) * w], F32, name="root" + name)
+            nc.scalar.activation(root[:], ms[:], ACT.Sqrt, bias=0.1)
+            for i, t in enumerate(tiles):
+                nc.scalar.activation(
+                    z_rows[:, t, v0:v1], root[:, i * w : (i + 1) * w], ACT.Copy, scale=gain[:, t : t + 1]
+                )
+
+        for t in range(WHOLE):
+            line_up([t], 0, V)
+        early, middle, late = spans(Z_CHUNKS)
+        chunked = list(range(WHOLE, PACK))
+
+        def weave(copy, woven, v0, v1):
+            copy(woven, z_rows[:, :, v0:v1].rearrange("p t v -> p v t"))
+
+        def quantise(woven, v0, v1):
+            nc.vector.quantize_mx(
+                out=z_codes[:, v0:v1].bitcast(FP8X4),
+                scales=z_plane[:, v0:v1],
+                in_=woven[:].rearrange("p v t -> p (v t)"),
+            )
+
+        half = early[1]
+        z_woven_first = keep.tile([P, half, PACK], BF16, align_bytes=64)
+        z_woven_second = ring.tile([P, V - half, PACK], BF16, align_bytes=64, offset=10240)
+        for t in chunked:
+            line_up([t], *early)
+        weave(nc.scalar.copy, z_woven_first[:], *early)
+        quantise(z_woven_first, *early)
+        line_up(chunked, *middle)
+        line_up(chunked, *late)
+        weave(nc.scalar.copy, z_woven_second[:, : middle[1] - half, :], *middle)
+        weave(nc.vector.tensor_copy, z_woven_second[:, late[0] - half :, :], *late)
+        quantise(z_woven_second, half, V)
 
         c_bytes_picked = ring.tile([P, C], U8, offset=8192)
-        c_plane = keep.tile([P, C], U8, align_bytes=64)
+        c_plane_first = keep.tile([P, P], U8, align_bytes=64)
         nc.vector.tensor_copy(c_bytes_picked[:], x_byte_win[:].indirect(cand_t[:]))
-        deal(c_plane, c_bytes_picked)
+        deal(c_plane_first, c_bytes_picked, 0, 1)
+        c_plane_rest = ring.tile([P, C - P], U8, align_bytes=64, offset=10240)
+        c_codes_rest = ring.tile([P, C - P], U32, align_bytes=64, offset=10240 + 512)
+        deal(c_plane_rest, c_bytes_picked, 1, PACK)
+        deal(c_codes_rest, c_words_picked, 1, PACK)
 
         out_rows = out_0.rearrange("(p t) v -> p t v", t=PACK)
         out_words = out_1[0].rearrange("p v t -> p (v t)").bitcast(I32)
         y = keep.tile([P, PACK, V], F32)
         y_codes = keep.tile([P, V], I32, align_bytes=64)
         y_plane = keep.tile([P, V], U8, align_bytes=64)
-        z_spans = spans(Z_CHUNKS)
         s_win, s_acc = [], []
         for t in range(PACK):
-            rows = slice(t * P, (t + 1) * P)
+            rows = slice((t - 1) * P, t * P)
+            c_codes = c_codes_rest[:, rows] if t else c_codes_first[:]
+            c_plane = c_plane_rest[:, rows] if t else c_plane_first[:]
             width = V if t == PACK - 1 else 2 * V
             if t == 0:
                 s_win.append(ring.tile([P, width], F32, name="s_win0", offset=0))
             else:
                 s_win.append(keep.tile([P, width], F32, name="s_win%d" % t))
             s_acc.append([])
-            for pieces in (z_spans[:-1], z_spans[-1:]) if t == 0 else ([(0, V)],):
+            for pieces in ([(0, half)], [(half, V)]) if t == 0 else ([(0, V)],):
                 first, last = pieces[0][0], pieces[-1][1]
                 pool = psum_h if t == 0 else psum_s
                 bank = pool.tile([P, BANK], F32, name="h_acc" if t == 0 else "s_acc")
                 for v0, v1 in pieces:
                     nc.tensor.matmul_mx(
                         out=bank[:, v0:v1],
-                        lhsT=c_codes[:, rows].bitcast(FP8X4),
-                        lhsT_scale=c_plane[:, rows],
+                        lhsT=c_codes.bitcast(FP8X4),
+                        lhsT_scale=c_plane,
                         rhs=z_codes[:, v0:v1].bitcast(FP8X4),
                         rhs_scale=z_plane[:, v0:v1],
                         start=True,
                         stop=True,
                     )
-                nc.scalar.activation(s_win[t][:, first:last], bank[:, first:last], ACT.Copy, scale=S_SCALE)
+                nc.scalar.activation(s_win[t][:, first:last], bank[:, first:last], ACT.Copy, scale=s_scale[:])
                 s_acc[t].append((bank, first, last))
 
-        def less(diff, fetched, t, v0, v1):
-            for bank, first, last in s_acc[t]:
-                a, b = max(first, v0), min(last, v1)
-                nc.vector.scalar_tensor_tensor(
-                    diff[:, a - v0 : b - v0], bank[:, a:b], S_SCALE, fetched[:, a - v0 : b - v0], ALU.mult, ALU.subtract
-                )
+        fused_from = Y_CHUNKS[0]
+        s_own = keep.tile([P, V - fused_from], F32)
+        nc.scalar.activation(s_own[:], s_acc[PACK - 1][0][0][:, fused_from:V], ACT.Copy, scale=s_scale[:])
 
         def differences(t, v0, v1):
-            at2, at3, diff2, diff3 = [
-                keep.tile([P, v1 - v0], F32, name="%s_%d_%d" % (name, t, v0)) for name in ("at2", "at3", "diff2", "diff3")
-            ]
-            nc.vector.tensor_copy(at3[:], s_win[t][:].indirect(entries(n3_t, v0, v1)))
-            nc.vector.tensor_copy(at2[:], s_win[t][:].indirect(entries(n2_t, v0, v1)))
-            if t == PACK - 1:
-                less(diff3, at3, t, v0, v1)
-                less(diff2, at2, t, v0, v1)
-            else:
-                less(diff3, at3, t, v0, v1)
-                nc.gpsimd.tensor_tensor(diff2[:], s_win[t][:, v0:v1], at2[:], ALU.subtract)
-            return diff2, diff3
+            made = []
+            for pos, name in ((n2_t, "2"), (n3_t, "3")):
+                diff = keep.tile([P, v1 - v0], F32, name="diff%s_%d_%d" % (name, t, v0))
+                looked_up = s_win[t][:].indirect(entries(pos, v0, v1))
+                made.append(diff)
+                if t == PACK - 1 and v0 >= fused_from:
+                    nc.vector.tensor_tensor(diff[:], looked_up, s_own[:, v0 - fused_from : v1 - fused_from], ALU.subtract)
+                    continue
+                fetched = keep.tile([P, v1 - v0], F32, name="fetched%s_%d_%d" % (name, t, v0))
+                nc.vector.tensor_copy(fetched[:], looked_up)
+                if t == 0 or (t < PACK - 1 and pos is n2_t):
+                    nc.gpsimd.tensor_tensor(diff[:], s_win[t][:, v0:v1], fetched[:], ALU.subtract)
+                else:
+                    nc.vector.scalar_tensor_tensor(
+                        diff[:], s_acc[t][0][0][:, v0:v1], s_scale[:], fetched[:], ALU.mult, ALU.subtract
+                    )
+            return made
 
         def finish(t, v0, v1, diff2, diff3):
             engine = nc.vector if t == PACK - 1 else nc.gpsimd
@@ -218,8 +254,8 @@ def tile_picked_pqcprmsquad_none_po_kernel(
             nc.sync.dma_start(out_rows[:, t, v0:v1], y[:, t, v0:v1])
             if t == PACK - 1:
                 y_woven = keep.tile([P, v1 - v0, PACK], BF16, align_bytes=64, name="y_woven%d" % v0)
-                weave = nc.vector.tensor_copy if v1 == V else nc.scalar.copy
-                weave(y_woven[:], y[:, :, v0:v1].rearrange("p t v -> p v t"))
+                copy = nc.vector.tensor_copy if v1 == V else nc.scalar.copy
+                copy(y_woven[:], y[:, :, v0:v1].rearrange("p t v -> p v t"))
                 nc.vector.quantize_mx(
                     out=y_codes[:, v0:v1].bitcast(FP8X4),
                     scales=y_plane[:, v0:v1],

@@ -232,7 +232,14 @@ def tile_picked_pqcprmsquad_none_po_kernel(
         def differences(t, v0, v1):
             made = []
             for pos, name in ((n2_t, "2"), (n3_t, "3")):
-                diff = keep.tile([P, v1 - v0], F32, name="diff%s_%d_%d" % (name, t, v0))
+                label = "diff%s_%d_%d" % (name, t, v0)
+                if t == PACK - 2 and pos is n3_t:
+                    diff = ring.tile([P, V], F32, name=label, offset=12288)
+                elif t == PACK - 1 and v0 >= fused_from:
+                    place = 12288 + 8 * (v0 - fused_from) + 4 * (v1 - v0) * len(made)
+                    diff = ring.tile([P, v1 - v0], F32, name=label, offset=place)
+                else:
+                    diff = keep.tile([P, v1 - v0], F32, name=label)
                 looked_up = s_win[t][:].indirect(entries(pos, v0, v1))
                 made.append(diff)
                 if t == PACK - 1 and v0 >= fused_from:
@@ -240,16 +247,19 @@ def tile_picked_pqcprmsquad_none_po_kernel(
                     continue
                 fetched = keep.tile([P, v1 - v0], F32, name="fetched%s_%d_%d" % (name, t, v0))
                 nc.vector.tensor_copy(fetched[:], looked_up)
-                if t == 0 or (t < PACK - 1 and pos is n2_t):
+                if t < PACK - 1 and pos is n2_t:
                     nc.gpsimd.tensor_tensor(diff[:], s_win[t][:, v0:v1], fetched[:], ALU.subtract)
                 else:
-                    nc.vector.scalar_tensor_tensor(
-                        diff[:], s_acc[t][0][0][:, v0:v1], s_scale[:], fetched[:], ALU.mult, ALU.subtract
-                    )
+                    for bank, first, last in s_acc[t]:
+                        a, b = max(first, v0), min(last, v1)
+                        here = slice(a - v0, b - v0)
+                        nc.vector.scalar_tensor_tensor(
+                            diff[:, here], bank[:, a:b], s_scale[:], fetched[:, here], ALU.mult, ALU.subtract
+                        )
             return made
 
         def finish(t, v0, v1, diff2, diff3):
-            engine = nc.vector if t == PACK - 1 else nc.gpsimd
+            engine = nc.vector if t >= PACK - 2 else nc.gpsimd
             engine.tensor_tensor(y[:, t, v0:v1], diff2[:], diff3[:], ALU.mult)
             nc.sync.dma_start(out_rows[:, t, v0:v1], y[:, t, v0:v1])
             if t == PACK - 1:

from contextlib import ExitStack

import concourse.mybir as mybir

K, T, S, V, G, H, C = 512, 2048, 1024, 512, 2048, 512, 512
FLOPS = 2 * K * H * S + 2 * K * C * V

F32 = mybir.dt.float32
BF16 = mybir.dt.bfloat16
I32 = mybir.dt.int32
U32 = mybir.dt.uint32
U16 = mybir.dt.uint16
U8 = mybir.dt.uint8
FP8X4 = mybir.dt.float8_e4m3fn_x4
ACT = mybir.ActivationFunctionType
ALU = mybir.AluOpType

WHOLE = 2
TAIL = 64
P = 128
PACK = 4
BANK = 512
Z_CHUNKS = (256, 128, 128)
Y_CHUNKS = (256, 128, 128)


def spans(widths):
    starts = [sum(widths[:i]) for i in range(len(widths))]
    return [(a, a + w) for a, w in zip(starts, widths)]


def entries(offsets, first, last):
    return offsets[:, first // 16 : last // 16]


def tile_picked_pqcprmsquad_none_po_kernel(
    tc, x_words, x_scales, d_words, d_scales, gs, offs, k1, n1, cand, n2, n3, out_0, out_1, out_2
):
    nc = tc.nc
    with ExitStack() as ctx:
        lists = ctx.enter_context(tc.tile_pool(name="lists", bufs=1))
        keep = ctx.enter_context(tc.tile_pool(name="keep", bufs=1))
        ring = ctx.enter_context(tc.tile_pool(name="ring", bufs=1))
        psum_h = ctx.enter_context(tc.psum_pool(name="psum_h", bufs=4))
        psum_s = ctx.enter_context(tc.psum_pool(name="psum_s", bufs=3))

        def load_list(source, name):
            tile = lists.tile(list(source.shape), U16, name=name)
            nc.sync.dma_start(tile[:], source)
            return tile

        d_byte_win = keep.tile([P, G], U8, align_bytes=64)
        x_byte_win = keep.tile([P, T], U8, align_bytes=64)
        d_word_win = keep.tile([P, G], I32, align_bytes=64)
        x_word_win = keep.tile([P, T], I32, align_bytes=64)
        gain = keep.tile([P, PACK], F32)

        k1_t = load_list(k1, "k1_t")
        nc.sync.dma_start(
            d_byte_win[:].bitcast(I32),
            d_scales[0].bitcast(I32).unsqueeze(1).broadcast_to([16, 8, G // 4]),
        )
        offs_t = load_list(offs, "offs_t")
        for q in range(4):
            nc.sync.dma_start(
                x_byte_win[32 * q : 32 * q + 32, :].bitcast(I32),
                x_scales[0, 4 * q : 4 * q + 4, :].bitcast(I32).unsqueeze(0).broadcast_to([8, 4, T // 4]),
            )
        nc.sync.dma_start(d_word_win[:], d_words[0].rearrange("p n t -> p (n t)").bitcast(I32))
        cand_t = load_list(cand, "cand_t")
        n1_t = load_list(n1, "n1_t")
        nc.sync.dma_start(x_word_win[:], x_words[0].rearrange("p n t -> p (n t)").bitcast(I32))
        nc.sync.dma_start(gain[:], gs.rearrange("(p t) o -> p (t o)", t=PACK))
        n2_t = load_list(n2, "n2_t")
        n3_t = load_list(n3, "n3_t")

        s_scale_squared = keep.tile([P, 1], F32)
        s_scale = keep.tile([P, 1], F32)
        nc.vector.memset(s_scale_squared[:], 0.75 / 256)
        nc.scalar.activation(s_scale[:], s_scale_squared[:], ACT.Sqrt)

        def deal(dealt, picked, t0=0, t1=PACK):
            nc.vector.tensor_copy(
                dealt[:].rearrange("p (t h m) -> p h t m", h=2, m=P // 2),
                picked[:].rearrange("p (h m t) -> p h t m", h=2, t=PACK)[:, :, t0:t1, :],
            )

        d_bytes_picked = keep.tile([P, H], U8, align_bytes=64)
        d_bytes_dealt = keep.tile([P, H], U8, align_bytes=64)
        d_plane = keep.tile([P, H], U8, align_bytes=64)
        nc.vector.memset(d_plane[:].bitcast(I32), 0)
        nc.vector.tensor_copy(d_bytes_picked[:], d_byte_win[:].indirect(k1_t[:]))
        deal(d_bytes_dealt, d_bytes_picked)
        for r in range(4):
            nc.sync.dma_start(d_plane[r:P:32, :].bitcast(I32), d_bytes_dealt[8 * r : P : 32, :].bitcast(I32))

        tok_plane = keep.tile([P, S], U8, align_bytes=64)
        nc.vector.tensor_copy(tok_plane[:], x_byte_win[:].indirect(offs_t[:]))

        d_words_picked = keep.tile([P, H], U32, align_bytes=64)
        d_codes = keep.tile([P, H], U32, align_bytes=64)
        nc.vector.tensor_copy(d_words_picked[:], d_word_win[:].bitcast(U32).indirect(k1_t[:]))
        deal(d_codes, d_words_picked)

        sq_win = [keep.tile([P, S if t >= WHOLE else 2 * S], F32, name="sq_win%d" % t) for t in range(PACK)]
        halves = spans((BANK,) * (S // BANK))
        tok_codes = [keep.tile([P, BANK], U32, align_bytes=64, name="tok_codes%d" % a) for a, b in halves]
        for codes, (a, b) in zip(tok_codes, halves):
            nc.vector.tensor_copy(codes[:], x_word_win[:].bitcast(U32).indirect(entries(offs_t, a, b)))
        tails = []
        for t in range(PACK):
            rows = slice(t * P, (t + 1) * P)
            for codes, (a, b) in zip(tok_codes, halves):
                h_acc = psum_h.tile([P, BANK], F32, name="h_acc")
                nc.tensor.matmul_mx(
                    out=h_acc[:],
                    lhsT=d_codes[:, rows].bitcast(FP8X4),
                    lhsT_scale=d_plane[:, rows],
                    rhs=codes[:].bitcast(FP8X4),
                    rhs_scale=tok_plane[:, a:b],
                    start=True,
                    stop=True,
                )
                width = BANK - TAIL if t >= WHOLE and b == S else BANK
                nc.scalar.activation(sq_win[t][:, a : a + width], h_acc[:, :width], ACT.Square, scale=0.0625)
                if width < BANK:
                    tails.append((t, h_acc))
        for t, h_acc in tails:
            nc.scalar.activation(sq_win[t][:, S - TAIL :], h_acc[:, BANK - TAIL :], ACT.Square, scale=0.0625)

        c_words_picked = keep.tile([P, C], U32, align_bytes=64)
        c_codes_first = keep.tile([P, P], U32, align_bytes=64)
        nc.vector.tensor_copy(c_words_picked[:], x_word_win[:].bitcast(U32).indirect(cand_t[:]))
        deal(c_codes_first, c_words_picked, 0, 1)

        z_rows = ring.tile([P, PACK, V], BF16, offset=0)
        z_codes = keep.tile([P, V], U32, align_bytes=64)
        z_plane = keep.tile([P, V], U8, align_bytes=64)
        def line_up(tiles, v0, v1):
            w, last = v1 - v0, v1 == V and tiles[-1] == PACK - 1
            name = "%d_%d" % (tiles[0], v0)
            if last:
                lined = ring.tile([P, len(tiles), 2 * w], F32, name="lined_last", offset=8192)
            else:
                lined = keep.tile([P, len(tiles), 2 * w], F32, name="lined" + name)
            for i, t in enumerate(tiles):
                nc.vector.tensor_copy(lined[:, i, :], sq_win[t][:].indirect(entries(n1_t, 2 * v0, 2 * v1)))
            pairs = lined[:].rearrange("p t (v e) -> p (t v) e", e=2)
            ms = keep.tile([P, len(tiles) * w], F32, name="ms" + name)
            (nc.vector if last else nc.gpsimd).tensor_tensor(ms[:], pairs[:, :, 0], pairs[:, :, 1], ALU.add)
            root = keep.tile([P, len(tiles) * w], F32, name="root" + name)
            nc.scalar.activation(root[:], ms[:], ACT.Sqrt, bias=0.1)
            for i, t in enumerate(tiles):
                nc.scalar.activation(
                    z_rows[:, t, v0:v1], root[:, i * w : (i + 1) * w], ACT.Copy, scale=gain[:, t : t + 1]
                )

        for t in range(WHOLE):
            line_up([t], 0, V)
        early, middle, late = spans(Z_CHUNKS)
        chunked = list(range(WHOLE, PACK))

        def weave(copy, woven, v0, v1):
            copy(woven, z_rows[:, :, v0:v1].rearrange("p t v -> p v t"))

        def quantise(woven, v0, v1):
            nc.vector.quantize_mx(
                out=z_codes[:, v0:v1].bitcast(FP8X4),
                scales=z_plane[:, v0:v1],
                in_=woven[:].rearrange("p v t -> p (v t)"),
            )

        half = early[1]
        z_woven_first = keep.tile([P, half, PACK], BF16, align_bytes=64)
        z_woven_second = ring.tile([P, V - half, PACK], BF16, align_bytes=64, offset=10240)
        for t in chunked:
            line_up([t], *early)
        weave(nc.scalar.copy, z_woven_first[:], *early)
        quantise(z_woven_first, *early)
        line_up(chunked, *middle)
        line_up(chunked, *late)
        weave(nc.scalar.copy, z_woven_second[:, : middle[1] - half, :], *middle)
        weave(nc.vector.tensor_copy, z_woven_second[:, late[0] - half :, :], *late)
        quantise(z_woven_second, half, V)

        c_bytes_picked = ring.tile([P, C], U8, offset=8192)
        c_plane_first = keep.tile([P, P], U8, align_bytes=64)
        nc.vector.tensor_copy(c_bytes_picked[:], x_byte_win[:].indirect(cand_t[:]))
        deal(c_plane_first, c_bytes_picked, 0, 1)
        c_plane_rest = ring.tile([P, C - P], U8, align_bytes=64, offset=10240)
        c_codes_rest = ring.tile([P, C - P], U32, align_bytes=64, offset=10240 + 512)
        deal(c_plane_rest, c_bytes_picked, 1, PACK)
        deal(c_codes_rest, c_words_picked, 1, PACK)

        out_rows = out_0.rearrange("(p t) v -> p t v", t=PACK)
        out_words = out_1[0].rearrange("p v t -> p (v t)").bitcast(I32)
        y = keep.tile([P, PACK, V], F32)
        y_codes = keep.tile([P, V], I32, align_bytes=64)
        y_plane = keep.tile([P, V], U8, align_bytes=64)
        s_win, s_acc = [], []
        for t in range(PACK):
            rows = slice((t - 1) * P, t * P)
            c_codes = c_codes_rest[:, rows] if t else c_codes_first[:]
            c_plane = c_plane_rest[:, rows] if t else c_plane_first[:]
            width = V if t == PACK - 1 else 2 * V
            if t == 0:
                s_win.append(ring.tile([P, width], F32, name="s_win0", offset=0))
            else:
                s_win.append(keep.tile([P, width], F32, name="s_win%d" % t))
            s_acc.append([])
            for pieces in ([(0, half)], [(half, V)]) if t == 0 else ([(0, V)],):
                first, last = pieces[0][0], pieces[-1][1]
                pool = psum_h if t == 0 else psum_s
                bank = pool.tile([P, BANK], F32, name="h_acc" if t == 0 else "s_acc")
                for v0, v1 in pieces:
                    nc.tensor.matmul_mx(
                        out=bank[:, v0:v1],
                        lhsT=c_codes.bitcast(FP8X4),
                        lhsT_scale=c_plane,
                        rhs=z_codes[:, v0:v1].bitcast(FP8X4),
                        rhs_scale=z_plane[:, v0:v1],
                        start=True,
                        stop=True,
                    )
                nc.scalar.activation(s_win[t][:, first:last], bank[:, first:last], ACT.Copy, scale=s_scale[:])
                s_acc[t].append((bank, first, last))

        fused_from = Y_CHUNKS[0]
        s_own = keep.tile([P, V - fused_from], F32)
        nc.scalar.activation(s_own[:], s_acc[PACK - 1][0][0][:, fused_from:V], ACT.Copy, scale=s_scale[:])

        def differences(t, v0, v1):
            made = []
            for pos, name in ((n2_t, "2"), (n3_t, "3")):
                label = "diff%s_%d_%d" % (name, t, v0)
                if t == PACK - 2 and pos is n3_t:
                    diff = ring.tile([P, V], F32, name=label, offset=12288)
                elif t == PACK - 1 and v0 >= fused_from:
                    place = 12288 + 8 * (v0 - fused_from) + 4 * (v1 - v0) * len(made)
                    diff = ring.tile([P, v1 - v0], F32, name=label, offset=place)
                else:
                    diff = keep.tile([P, v1 - v0], F32, name=label)
                looked_up = s_win[t][:].indirect(entries(pos, v0, v1))
                made.append(diff)
                if t == PACK - 1 and v0 >= fused_from:
                    nc.vector.tensor_tensor(diff[:], looked_up, s_own[:, v0 - fused_from : v1 - fused_from], ALU.subtract)
                    continue
                fetched = keep.tile([P, v1 - v0], F32, name="fetched%s_%d_%d" % (name, t, v0))
                nc.vector.tensor_copy(fetched[:], looked_up)
                if t < PACK - 1 and pos is n2_t:
                    nc.gpsimd.tensor_tensor(diff[:], s_win[t][:, v0:v1], fetched[:], ALU.subtract)
                else:
                    for bank, first, last in s_acc[t]:
                        a, b = max(first, v0), min(last, v1)
                        here = slice(a - v0, b - v0)
                        nc.vector.scalar_tensor_tensor(
                            diff[:, here], bank[:, a:b], s_scale[:], fetched[:, here], ALU.mult, ALU.subtract
                        )
            return made

        def finish(t, v0, v1, diff2, diff3):
            engine = nc.vector if t >= PACK - 2 else nc.gpsimd
            engine.tensor_tensor(y[:, t, v0:v1], diff2[:], diff3[:], ALU.mult)
            nc.sync.dma_start(out_rows[:, t, v0:v1], y[:, t, v0:v1])
            if t == PACK - 1:
                y_woven = keep.tile([P, v1 - v0, PACK], BF16, align_bytes=64, name="y_woven%d" % v0)
                copy = nc.vector.tensor_copy if v1 == V else nc.scalar.copy
                copy(y_woven[:], y[:, :, v0:v1].rearrange("p t v -> p v t"))
                nc.vector.quantize_mx(
                    out=y_codes[:, v0:v1].bitcast(FP8X4),
                    scales=y_plane[:, v0:v1],
                    in_=y_woven[:].rearrange("p v t -> p (v t)"),
                )
                nc.sync.dma_start(out_words[:, v0:v1], y_codes[:, v0:v1])

        steps = [(t, 0, V) for t in range(PACK - 1)] + [(PACK - 1, v0, v1) for v0, v1 in spans(Y_CHUNKS)]
        pending = None
        for step in steps:
            diffs = differences(*step)
            if pending:
                finish(*pending)
            pending = (*step, *diffs)
        finish(*pending)
        for q in range(4):
            queue = nc.sync if q % 2 else nc.scalar
            queue.dma_start(out_2[0, 4 * q : 4 * q + 4, :].bitcast(I32), y_plane[32 * q : 32 * q + 4, :].bitcast(I32))
